import numpy as np, ml_dtypes
CORES = [9,41,49,65,73,81,97,113,15,47,55,71,79,87,103,119]
N = 16
T = 2048
def entries(a): return a.T.reshape(-1)
def pack(v, P): return np.ascontiguousarray(np.asarray(v, np.int32).reshape(-1, P).T)
def lists(rng, how):
    h = rng.integers(0, N * T, 8)
    if how == "zero": h[:] = 0
    if how == "blocks": h = T * rng.integers(1, N, 8)
    if how == "last": h[:] = N * T - 1
    if how == "mixed": h = T * rng.choice([q for q in range(N) if q & (q - 1)], 8) + rng.integers(1, T, 8)
    if how == "small": h = rng.integers(1, T, 8)
    h[1:] = 0
    return {"hh": np.broadcast_to(pack(np.concatenate([h, np.zeros(24, np.int64)]), 16), (N, 16, 2)).copy()}
def setup_inputs(rng):
    return dict({"x": rng.standard_normal((N, 128, T), dtype=np.float32).astype(ml_dtypes.bfloat16)}, **lists(rng, "uniform"))
def setup_inputs_blocks(rng):
    d = setup_inputs(rng); d.update(lists(rng, "blocks"))
    for k in ("x",): d[k] = (d[k].astype(np.float32) * 1048576.0).astype(d[k].dtype)
    return d
def setup_inputs_last(rng):
    d = setup_inputs(rng); d.update(lists(rng, "last"))
    for k in ("x",): d[k] = (d[k].astype(np.float32) * (1 / 1024.0)).astype(d[k].dtype)
    return d
def setup_inputs_mixed(rng):
    d = setup_inputs(rng); d.update(lists(rng, "mixed"))
    return d
def setup_inputs_small(rng):
    d = setup_inputs(rng); d.update(lists(rng, "small"))
    return d
def setup_inputs_zero(rng):
    d = setup_inputs(rng); d.update(lists(rng, "zero"))
    return d
def check_inputs(x):
    bad = []
    if x["hh"].min() < 0 or x["hh"].max() >= N * T: bad.append("hh out of range")
    if entries(x["hh"][0])[1:].any(): bad.append("an entry that should be 0 isn't")
    if not all(np.array_equal(a, x["hh"][0]) for a in x["hh"]): bad.append("hh isn't alike on all ranks")
    return bad
def reference(x, hh):
    h = entries(hh[0]); A = np.concatenate(list(x), axis=1)
    Y = np.roll(A, -int(h[0]), axis=1)
    return {"y": np.stack([Y[:, T * r:T * r + T] for r in range(N)])}

@@ -1,0 +1,287 @@
+from concourse.bass import DstId, RemoteDMATransfer
+from concourse.mybir import AluOpType, ActivationFunctionType
+
+NR = 16
+COLS = 2048
+W = COLS // NR
+OC = W // 16
+
+SCRATCH = {
+    "xs": ("sbuf", [128, COLS], "bfloat16"),
+    "rot": ("sbuf", [128, COLS], "bfloat16"),
+    "rel": ("sbuf", [128, COLS], "bfloat16"),
+    "win": ("sbuf", [128, COLS], "bfloat16"),
+    "sel": ("sbuf", [128, COLS], "bfloat16"),
+    "land": ("sbuf", [128, COLS], "bfloat16"),
+    "h1": ("sbuf", [128, 2], "int32"),
+    "hb": ("sbuf", [128, 2], "int32"),
+    "hf": ("sbuf", [128, 1], "float32"),
+    "pi": ("sbuf", [128, 1], "int32"),
+    "pj": ("sbuf", [128, 1], "int32"),
+    "pf": ("sbuf", [128, 1], "float32"),
+    "ia": ("sbuf", [128, NR * OC], "int32"),
+    "ib": ("sbuf", [128, NR * OC], "int32"),
+    "ic": ("sbuf", [128, NR * OC], "int32"),
+    "id_": ("sbuf", [128, NR * OC], "int32"),
+    "ie": ("sbuf", [128, NR * OC], "int32"),
+    "it": ("sbuf", [128, NR * OC], "int32"),
+    "iu": ("sbuf", [128, NR * OC], "int32"),
+    "off": ("sbuf", [128, NR * OC], "uint16"),
+}
+SEMAPHORES = ["xl", "hl", "pb", "iop", "ioa", "iot", "vc", "ga", "gb", "gc_", "rl", "hland", "rland", "wland",
+              "z0", "z1", "st"]
+
+
+def bits(m):
+    return [1 << i for i in range(m.bit_length()) if (m >> i) & 1]
+
+
+def deal(engines, n):
+    k = len(engines) // n
+    return [sum(engines[i * k:(i + 1) * k]) for i in range(n)]
+
+
+def halves(n):
+    return [1 << i for i in range(n.bit_length() - 1, -1, -1) if (n >> i) & 1]
+
+
+def layout(T, topo):
+    cores = list(T.cores)
+    chips = sorted({topo.chip(c) for c in cores})
+    planes = []
+    for ch in chips:
+        for p in planes:
+            if topo.same_plane(ch, p[0]):
+                p.append(ch)
+                break
+        else:
+            planes.append([ch])
+    order = [ch for p in planes for ch in p]
+    rank_core = [c for ch in order for c in cores if topo.chip(c) == ch]
+    inter, second = [], []
+    for c in rank_core:
+        own = [d for d in range(topo.CHIPS * topo.CORES_PER_CHIP)
+               if topo.chip(d) == topo.chip(c) and topo.die(d) == topo.die(c) and d not in cores
+               and all(topo.may_write(d, r) for r in cores)]
+        inter.append(own[0])
+        second.append(own[1] if len(own) > 1 else None)
+    return rank_core, inter, second
+
+
+def engines(topo, core, rank_core):
+    off = bits(topo.mask(core, next(c for c in rank_core if topo.chip(c) != topo.chip(core))))
+    on = bits(topo.mask(core, next(c for c in rank_core if topo.chip(c) == topo.chip(core) and c != core)))
+    return off, [e for e in on if e not in off]
+
+
+def phase1(topo, pos, rank_core, inter, second):
+    core = rank_core[pos]
+    low, high = engines(topo, core, rank_core)
+    home = [p for p in range(NR) if topo.chip(rank_core[p]) == topo.chip(core)]
+    barred = [p for p in range(NR) if not topo.may_write(core, inter[p])]
+    if barred:
+        start = next(p for p in barred if (p - 1) % NR not in barred)
+        n = len(barred)
+        a = n // 2
+        relays = [(inter[pos], 0, a, sum(low)), (second[pos], a, n - a, sum(high))]
+        idx = range(n, NR)
+        on = [i for i in idx if (start + i) % NR in home]
+        off = [i for i in idx if i not in on]
+        calls = [list(zip(off, deal(low, len(off)))) + list(zip(on, deal(high, len(on))))]
+        m = (n + NR) // 2
+        gathers = [[(0, a), (a, n)], [(n, m), (m, NR)]]
+    else:
+        start = home[0]
+        relays = [(inter[pos], 2, 4, sum(high))]
+        calls = [list(zip([6, 7], deal(low, 2))) + list(zip([0, 1], deal(high, 2))),
+                 list(zip(range(8, 16), deal(low, 8)))]
+        gathers = [[(2, 4), (4, 6)], [(6, 8), (0, 2)], [(8, 12), (12, 16)]]
+    return start, relays, calls, gathers
+
+
+def relay_calls(topo, helper, first, n, rank_core):
+    low, _high = engines(topo, helper, rank_core)
+    calls, i = [], first
+    for k in halves(n):
+        calls.append(list(zip(range(i, i + k), deal(low, k))))
+        i += k
+    return calls
+
+
+def phase2(topo, pos, rank_core, inter):
+    low, high = engines(topo, inter[pos], rank_core)
+    start = next(p for p in range(NR) if topo.chip(rank_core[p]) == topo.chip(rank_core[pos]))
+    calls = [list(zip([2, 3], deal(low, 2))) + list(zip([0, 1], deal(high, 2))),
+             list(zip(range(4, 8), deal(low, 4))),
+             list(zip(range(8, 16), deal(low, 8)))]
+    return start, calls
+
+
+def count(mask):
+    return len(bits(mask))
+
+
+def cols(t, i, n=1):
+    return t[:, i * W:(i + n) * W]
+
+
+def rank_program(g, core, T, topo):
+    rank_core, inter, second = layout(T, topo)
+    rank_at = [T.rank_of(c) for c in rank_core]
+    S = T.sem
+
+    def xfer(dst_core, mask, sem, src, dst):
+        rid, pid, _ = topo.addr(dst_core)
+        return RemoteDMATransfer(dst_ids=[DstId(rid=rid, pnc=pid)], dma_engine_mask=mask, remote_sem=sem,
+                                 src=src, dst=dst)
+
+    def lane():
+        g.vector.wait_ge(S.iop, 1)
+        g.vector.tensor_scalar(T.pj[:], T.pi[:], 15, None, AluOpType.bitwise_and).then_inc(S.vc, 1)
+        g.vector.wait_ge(S.vc, 1)
+        g.vector.tensor_copy(T.pf[:], T.pj[:]).then_inc(S.vc, 1)
+
+    def gather(queue, out, src, a, b, sem):
+        ind = src[:, :].indirect(T.off[:, a * OC:b * OC])
+        if queue == 0:
+            g.vector.tensor_copy(out[:, a * W:b * W], ind).then_inc(sem, 1)
+        else:
+            g.scalar.activation(out[:, a * W:b * W], ind, ActivationFunctionType.Copy).then_inc(sem, 1)
+
+    gsem = [S.ga, S.gb, S["gc_"]]
+
+    if core in rank_core:
+        pos = rank_core.index(core)
+        mu = inter[pos]
+        start, relays, calls, gathers = phase1(topo, pos, rank_core, inter, second)
+        low, high = engines(topo, core, rank_core)
+        g.sync.dma_start(T.xs[:], T.x[:]).then_inc(S.xl, 16)
+        g.scalar.dma_start(T.h1[0:1, 0:2], T.hh[0:1, 0:2]).then_inc(S.hl, 16)
+        g.iota(T.pi[:], [[0, 1]], 0, 1).then_inc(S.iop, 1)
+        g.iota(T.ia[:], [[16, NR * OC]], start * W, 0).then_inc(S.ioa, 1)
+        g.wait_ge(S.hl, 16)
+        g.partition_broadcast(T.hb[:], T.h1[0:1, 0:2], 128).then_inc(S.pb, 1)
+        g.wait_ge(S.pb, 1)
+        rid, pid, _ = topo.addr(mu)
+        g.remote_dma(T.hb[:], T.hb[:], S.hland, S.rl, pid, rid, topo.mask(core, mu))
+        sent = count(topo.mask(core, mu))
+        lane()
+        g.vector.wait_ge(S.pb, 1)
+        g.vector.tensor_copy(T.hf[:], T.hb[:, 0:1]).then_inc(S.vc, 1)
+        g.vector.wait_ge(S.vc, 3)
+        g.vector.wait_ge(S.ioa, 1)
+        g.vector.tensor_scalar(T.ib[:], T.ia[:], T.pf[:], T.hf[:], AluOpType.add, AluOpType.add).then_inc(S.vc, 1)
+        g.vector.wait_ge(S.vc, 4)
+        g.vector.tensor_scalar(T.ic[:], T.ib[:], COLS - 1, None, AluOpType.bitwise_and).then_inc(S.vc, 1)
+        g.vector.wait_ge(S.vc, 5)
+        g.vector.tensor_copy(T.off[:], T.ic[:]).then_inc(S.vc, 1)
+        for k, q in enumerate((g.vector, g.scalar)):
+            q.wait_ge(S.vc, 6)
+            q.wait_ge(S.xl, 16)
+            for st, pair in enumerate(gathers):
+                gather(k, T.rot, T.xs, pair[k][0], pair[k][1], gsem[st])
+        g.wait_ge(gsem[0], 2)
+        widths = sorted({n for _, _, n, _ in relays})
+        for n in widths:
+            tr = [xfer(d, m, S.rland, cols(T.rot, i, n), cols(T.rel, 0, n)) for d, i, nn, m in relays if nn == n]
+            g.remote_dma_fused(tr, local_sem=S.rl)
+        sent += sum(count(m) for _, _, _, m in relays)
+        slot = T.rank_of(core)
+        for st, call in enumerate(calls):
+            g.wait_ge(gsem[st + 1], 2)
+            g.remote_dma_fused([xfer(inter[(start + i) % NR], m, S.wland, cols(T.rot, i), cols(T.win, slot))
+                                for i, m in call], local_sem=S.rl)
+            sent += sum(count(m) for _, m in call)
+        need = [0, 0]
+        half = [[], []]
+        for p in range(NR):
+            s2, c2 = phase2(topo, p, rank_core, inter)
+            for st, call in enumerate(c2):
+                for i, m in call:
+                    if (s2 + i) % NR == pos:
+                        h = 0 if st < 2 else 1
+                        need[h] += count(m)
+                        half[h].append(p)
+        stores = 0
+        for h in range(2):
+            runs = []
+            for p in half[h]:
+                if runs and runs[-1][1] == p:
+                    runs[-1][1] = p + 1
+                else:
+                    runs.append([p, p + 1])
+            if len(runs) == 1:
+                a, b = runs[0]
+                runs = [[a, (a + b) // 2], [(a + b) // 2, b]]
+            for k, (a, b) in enumerate(runs):
+                q = (g.sync, g.scalar)[k % 2]
+                q.wait_ge((S.z0, S.z1)[h], need[h])
+                q.dma_start(T.y[:, a * W:b * W], T.land[:, a * W:b * W]).then_inc(S.st, 16)
+                stores += 16
+        g.wait_ge(S.rl, sent)
+        g.sync.wait_ge(S.st, stores)
+        return
+
+    jobs = []
+    if core in inter or core in second:
+        for p in range(NR):
+            for d, i, n, m in phase1(topo, p, rank_core, inter, second)[1]:
+                if d == core:
+                    jobs.append((p, i, n, m))
+    if not jobs and core not in inter:
+        return
+    sent = 0
+    if core in inter:
+        pos = inter.index(core)
+        start2, calls2 = phase2(topo, pos, rank_core, inter)
+        g.iota(T.pi[:], [[0, 1]], 0, 1).then_inc(S.iop, 1)
+        g.iota(T.it[:], [[0, NR], [16, OC]], 0, 0).then_inc(S.iot, 1)
+        for i in range(NR):
+            b = rank_at[(start2 + i) % NR]
+            g.iota(T.ia[:, i * OC:(i + 1) * OC], [[16, OC]], COLS * b + W * pos, 0).then_inc(S.ioa, 1)
+        lane()
+        v = g.vector
+        v.wait_ge(S.hland, count(topo.mask(rank_core[pos], core)))
+        v.tensor_copy(T.hf[:], T.hb[:, 0:1]).then_inc(S.vc, 1)
+        v.wait_ge(S.iot, 1)
+        v.wait_ge(S.vc, 3)
+        v.tensor_scalar(T.iu[:], T.it[:], T.pf[:], None, AluOpType.add).then_inc(S.vc, 1)
+        v.wait_ge(S.ioa, NR)
+        v.wait_ge(S.vc, 4)
+        v.tensor_scalar(T.ib[:], T.ia[:], T.pf[:], T.hf[:], AluOpType.add, AluOpType.add).then_inc(S.vc, 1)
+        v.wait_ge(S.vc, 5)
+        v.tensor_scalar(T.ic[:], T.ib[:], 11, NR - 1, AluOpType.logical_shift_right,
+                        AluOpType.bitwise_and).then_inc(S.vc, 1)
+        v.wait_ge(S.vc, 6)
+        v.tensor_scalar(T["id_"][:], T.ic[:], float(W), None, AluOpType.mult).then_inc(S.vc, 1)
+        v.wait_ge(S.vc, 7)
+        v.tensor_tensor(T.ie[:], T["id_"][:], T.iu[:], AluOpType.add).then_inc(S.vc, 1)
+        v.wait_ge(S.vc, 8)
+        v.tensor_copy(T.off[:], T.ie[:]).then_inc(S.vc, 1)
+        need = 0
+        for p in range(NR):
+            s1, rl1, c1, _ = phase1(topo, p, rank_core, inter, second)
+            todo = [c for c in c1]
+            for d, i, n, _m in rl1:
+                todo += relay_calls(topo, d, i, n, rank_core)
+            need += sum(count(m) for c in todo for i, m in c if (s1 + i) % NR == pos)
+        for k, q in enumerate((g.vector, g.scalar)):
+            q.wait_ge(S.vc, 9)
+            q.wait_ge(S.wland, need)
+            for st, (a, b) in enumerate(((0, 4), (4, 8), (8, 16))):
+                mid = (a + b) // 2
+                gather(k, T.sel, T.win, (a, mid)[k], (mid, b)[k], gsem[st])
+    for p, first, n, mask in jobs:
+        g.wait_ge(S.rland, count(mask))
+        s1 = phase1(topo, p, rank_core, inter, second)[0]
+        for call in relay_calls(topo, core, first, n, rank_core):
+            g.remote_dma_fused([xfer(inter[(s1 + i) % NR], m, S.wland, cols(T.rel, i - first), cols(T.win, rank_at[p]))
+                                for i, m in call], local_sem=S.rl)
+            sent += sum(count(m) for _, m in call)
+    if core in inter:
+        for st, call in enumerate(calls2):
+            g.wait_ge(gsem[st], 2)
+            g.remote_dma_fused([xfer(rank_core[(start2 + i) % NR], m, (S.z0, S.z1)[0 if st < 2 else 1],
+                                     cols(T.sel, i), cols(T.land, pos)) for i, m in call], local_sem=S.rl)
+            sent += sum(count(m) for _, m in call)
+    g.wait_ge(S.rl, sent)

@@ -2,16 +2,20 @@ from concourse.bass import DstId, RemoteDMATransfer
 from concourse.mybir import AluOpType, ActivationFunctionType
 
 NR = 16
+NI = 32
 COLS = 2048
-W = COLS // NR
+W = COLS // NI
 OC = W // 16
+K = NR * OC
+RELAY = 8
+STEPS = 4
 
 SCRATCH = {
     "xs": ("sbuf", [128, COLS], "bfloat16"),
     "rot": ("sbuf", [128, COLS], "bfloat16"),
     "rel": ("sbuf", [128, COLS], "bfloat16"),
-    "win": ("sbuf", [128, COLS], "bfloat16"),
-    "sel": ("sbuf", [128, COLS], "bfloat16"),
+    "win": ("sbuf", [128, NR * W], "bfloat16"),
+    "sel": ("sbuf", [128, NR * W], "bfloat16"),
     "land": ("sbuf", [128, COLS], "bfloat16"),
     "h1": ("sbuf", [128, 2], "int32"),
     "hb": ("sbuf", [128, 2], "int32"),
@@ -19,21 +23,30 @@ SCRATCH = {
     "pi": ("sbuf", [128, 1], "int32"),
     "pj": ("sbuf", [128, 1], "int32"),
     "pf": ("sbuf", [128, 1], "float32"),
-    "ia": ("sbuf", [128, NR * OC], "int32"),
-    "ib": ("sbuf", [128, NR * OC], "int32"),
-    "ic": ("sbuf", [128, NR * OC], "int32"),
-    "id_": ("sbuf", [128, NR * OC], "int32"),
-    "ie": ("sbuf", [128, NR * OC], "int32"),
-    "it": ("sbuf", [128, NR * OC], "int32"),
-    "iu": ("sbuf", [128, NR * OC], "int32"),
-    "off": ("sbuf", [128, NR * OC], "uint16"),
+    "ia": ("sbuf", [128, COLS // 16], "int32"),
+    "ib": ("sbuf", [128, COLS // 16], "int32"),
+    "ic": ("sbuf", [128, COLS // 16], "int32"),
+    "id_": ("sbuf", [128, K], "int32"),
+    "ie": ("sbuf", [128, K], "int32"),
+    "it": ("sbuf", [128, K], "int32"),
+    "iu": ("sbuf", [128, K], "int32"),
+    "tab": ("sbuf", [128, K], "int32"),
+    "off": ("sbuf", [128, COLS // 16], "uint16"),
 }
-SEMAPHORES = ["xl", "hl", "pb", "iop", "ioa", "iot", "vc", "ga", "gb", "gc_", "rl", "hland", "rland", "wland",
-              "z0", "z1", "st"]
+SEMAPHORES = ["xl", "hl", "pb", "iop", "ioa", "iot", "vc", "tm", "tland", "rl", "hland", "rland", "wland", "st",
+              "g0", "g1", "g2", "g3", "g4", "z0", "z1", "z2", "z3"]
 
 
 def bits(m):
     return [1 << i for i in range(m.bit_length()) if (m >> i) & 1]
+
+
+def count(mask):
+    return len(bits(mask))
+
+
+def pow2(n):
+    return 1 << (n - 1).bit_length()
 
 
 def deal(engines, n):
@@ -41,15 +54,28 @@ def deal(engines, n):
     return [sum(engines[i * k:(i + 1) * k]) for i in range(n)]
 
 
-def halves(n):
-    return [1 << i for i in range(n.bit_length() - 1, -1, -1) if (n >> i) & 1]
+def runs(idx):
+    out = []
+    for i in sorted(idx):
+        if out and out[-1][1] == i:
+            out[-1][1] = i + 1
+        else:
+            out.append([i, i + 1])
+    return out
+
+
+def cols(t, i, n=1):
+    return t[:, i * W:(i + n) * W]
+
+
+def all_cores(topo):
+    return range(topo.CHIPS * topo.CORES_PER_CHIP)
 
 
 def layout(T, topo):
     cores = list(T.cores)
-    chips = sorted({topo.chip(c) for c in cores})
     planes = []
-    for ch in chips:
+    for ch in range(topo.CHIPS):
         for p in planes:
             if topo.same_plane(ch, p[0]):
                 p.append(ch)
@@ -58,82 +84,129 @@ def layout(T, topo):
             planes.append([ch])
     order = [ch for p in planes for ch in p]
     rank_core = [c for ch in order for c in cores if topo.chip(c) == ch]
-    inter, second = [], []
-    for c in rank_core:
-        own = [d for d in range(topo.CHIPS * topo.CORES_PER_CHIP)
-               if topo.chip(d) == topo.chip(c) and topo.die(d) == topo.die(c) and d not in cores
-               and all(topo.may_write(d, r) for r in cores)]
-        inter.append(own[0])
-        second.append(own[1] if len(own) > 1 else None)
-    return rank_core, inter, second
+    dies = sorted({topo.die(c) for c in all_cores(topo)}, reverse=True)
+    inter = [next(c for c in all_cores(topo) if topo.chip(c) == ch and topo.die(c) == d and c not in cores
+                  and all(topo.may_write(c, r) for r in cores)) for ch in order for d in dies]
+    return rank_core, inter
 
 
-def engines(topo, core, rank_core):
-    off = bits(topo.mask(core, next(c for c in rank_core if topo.chip(c) != topo.chip(core))))
-    on = bits(topo.mask(core, next(c for c in rank_core if topo.chip(c) == topo.chip(core) and c != core)))
+def engines(topo, core):
+    on = bits(topo.mask(core, next(c for c in all_cores(topo) if topo.chip(c) == topo.chip(core) and c != core)))
+    off = bits(topo.mask(core, next(c for c in all_cores(topo) if topo.same_plane(topo.chip(c), topo.chip(core)))))
     return off, [e for e in on if e not in off]
 
 
-def phase1(topo, pos, rank_core, inter, second):
-    core = rank_core[pos]
-    low, high = engines(topo, core, rank_core)
-    home = [p for p in range(NR) if topo.chip(rank_core[p]) == topo.chip(core)]
-    barred = [p for p in range(NR) if not topo.may_write(core, inter[p])]
-    if barred:
-        start = next(p for p in barred if (p - 1) % NR not in barred)
-        n = len(barred)
-        a = n // 2
-        relays = [(inter[pos], 0, a, sum(low)), (second[pos], a, n - a, sum(high))]
-        idx = range(n, NR)
-        on = [i for i in idx if (start + i) % NR in home]
-        off = [i for i in idx if i not in on]
-        calls = [list(zip(off, deal(low, len(off)))) + list(zip(on, deal(high, len(on))))]
-        m = (n + NR) // 2
-        gathers = [[(0, a), (a, n)], [(n, m), (m, NR)]]
-    else:
-        start = home[0]
-        relays = [(inter[pos], 2, 4, sum(high))]
-        calls = [list(zip([6, 7], deal(low, 2))) + list(zip([0, 1], deal(high, 2))),
-                 list(zip(range(8, 16), deal(low, 8)))]
-        gathers = [[(2, 4), (4, 6)], [(6, 8), (0, 2)], [(8, 12), (12, 16)]]
-    return start, relays, calls, gathers
-
-
-def relay_calls(topo, helper, first, n, rank_core):
-    low, _high = engines(topo, helper, rank_core)
-    calls, i = [], first
-    for k in halves(n):
-        calls.append(list(zip(range(i, i + k), deal(low, k))))
-        i += k
+def calls_for(topo, core, dst, idx, sizes):
+    low, high = engines(topo, core)
+    on = [i for i in idx if topo.chip(dst(i)) == topo.chip(core)]
+    off = [i for i in idx if i not in on]
+    calls, k = [], 0
+    for s in sizes(len(off)):
+        calls.append(list(zip(off[k:k + s], deal(low, s))))
+        k += s
+    if on:
+        calls[0] += list(zip(on, deal(high, pow2(len(on)))))
     return calls
 
 
+def wide(n):
+    return [s for s in (1, 2, 4) if n & s] + [8] * (n // 8)
+
+
+def stepwise(n):
+    return ([n % 4] if n % 4 else []) + [4] * (n // 4)
+
+
+def phase1(topo, pos, rank_core, inter):
+    core = rank_core[pos]
+    chip = topo.chip(core)
+    low, high = engines(topo, core)
+    mine = [d for d in all_cores(topo) if topo.chip(d) == chip and topo.die(d) == topo.die(core)
+            and d not in rank_core]
+    full = [d for d in mine if all(topo.may_write(d, r) for r in rank_core)]
+    part = [d for d in mine if d not in full]
+    other = [p for p in range(NI) if topo.chip(inter[p]) != chip and not topo.same_plane(topo.chip(inter[p]), chip)]
+    barred = [p for p in range(NI) if not topo.may_write(core, inter[p])]
+    if barred:
+        start, n = barred[0], len(barred)
+        k = n // len(full)
+        parts = [(d, j * k, k) for j, d in enumerate(full)]
+    else:
+        start, n = other[-1] + 1 - RELAY, 2 * RELAY
+        parts = [(full[0], 0, RELAY), (part[0], RELAY, RELAY)]
+    relays = [(d, i, k, m) for (d, i, k), m in zip(parts, deal(low + high, len(parts)))]
+    return start, relays, n, calls_for(topo, core, lambda i: inter[(start + i) % NI], range(n, NI), wide)
+
+
+def relay_calls(topo, helper, start, first, n, inter):
+    return calls_for(topo, helper, lambda i: inter[(start + i) % NI], range(first, first + n), wide)
+
+
 def phase2(topo, pos, rank_core, inter):
-    low, high = engines(topo, inter[pos], rank_core)
-    start = next(p for p in range(NR) if topo.chip(rank_core[p]) == topo.chip(rank_core[pos]))
-    calls = [list(zip([2, 3], deal(low, 2))) + list(zip([0, 1], deal(high, 2))),
-             list(zip(range(4, 8), deal(low, 4))),
-             list(zip(range(8, 16), deal(low, 8)))]
-    return start, calls
+    chip = topo.chip(inter[pos])
+    key = [topo.chip(c) for c in rank_core]
+    if chip in key:
+        start = key.index(chip)
+    else:
+        idle = []
+        for m in inter:
+            if topo.chip(m) not in key and topo.chip(m) not in idle:
+                idle.append(topo.chip(m))
+        idle.sort()
+        start = idle.index(chip) * NR // len(idle)
+    return start, calls_for(topo, inter[pos], lambda i: rank_core[(start + i) % NR], range(NR), stepwise)
 
 
-def count(mask):
-    return len(bits(mask))
+def feeds(topo, rank_core, inter):
+    out = {c: [] for c in rank_core}
+    rest = []
+    for m in inter:
+        own = [c for c in rank_core if topo.chip(c) == topo.chip(m) and topo.die(c) == topo.die(m)]
+        if own:
+            out[own[0]].append(m)
+        else:
+            rest.append(m)
+    for m in rest:
+        able = [c for c in rank_core if topo.may_write(c, m)]
+        out[min(able, key=lambda c: (len(out[c]), all(topo.may_write(c, i) for i in inter)))].append(m)
+    for c in rank_core:
+        low, high = engines(topo, c)
+        on = [m for m in out[c] if topo.chip(m) == topo.chip(c)]
+        off = [m for m in out[c] if m not in on]
+        out[c] = list(zip(on, deal(high, pow2(len(on))))) + (list(zip(off, deal(low, pow2(len(off))))) if off else [])
+    return out
 
 
-def cols(t, i, n=1):
-    return t[:, i * W:(i + n) * W]
+def shares(topo, chip, rank_core, inter):
+    here = [c for c in inter if topo.chip(c) == chip]
+    who = set(here)
+    for p in range(NR):
+        who |= {d for d, _, _, _ in phase1(topo, p, rank_core, inter)[1] if topo.chip(d) == chip}
+    who = sorted(who)
+    return here, {c: (k * NR // len(who), (k + 1) * NR // len(who)) for k, c in enumerate(who)}
+
+
+def share_writes(topo, core, here):
+    to = [m for m in here if m != core]
+    return list(zip(to, deal(engines(topo, core)[0], len(to))))
 
 
 def rank_program(g, core, T, topo):
-    rank_core, inter, second = layout(T, topo)
+    rank_core, inter = layout(T, topo)
     rank_at = [T.rank_of(c) for c in rank_core]
     S = T.sem
+    gsem = [S["g%d" % k] for k in range(5)]
+    zsem = [S["z%d" % k] for k in range(STEPS)]
+    sent = [0]
 
-    def xfer(dst_core, mask, sem, src, dst):
-        rid, pid, _ = topo.addr(dst_core)
-        return RemoteDMATransfer(dst_ids=[DstId(rid=rid, pnc=pid)], dma_engine_mask=mask, remote_sem=sem,
-                                 src=src, dst=dst)
+    def fused(parts, sem, src, dst):
+        tr = []
+        for d, mask, k in parts:
+            rid, pid, _ = topo.addr(d)
+            tr.append(RemoteDMATransfer(dst_ids=[DstId(rid=rid, pnc=pid)], dma_engine_mask=mask, remote_sem=sem,
+                                        src=src(k), dst=dst(k)))
+            sent[0] += count(mask)
+        g.remote_dma_fused(tr, local_sem=S.rl)
 
     def lane():
         g.vector.wait_ge(S.iop, 1)
@@ -141,147 +214,138 @@ def rank_program(g, core, T, topo):
         g.vector.wait_ge(S.vc, 1)
         g.vector.tensor_copy(T.pf[:], T.pj[:]).then_inc(S.vc, 1)
 
-    def gather(queue, out, src, a, b, sem):
-        ind = src[:, :].indirect(T.off[:, a * OC:b * OC])
-        if queue == 0:
-            g.vector.tensor_copy(out[:, a * W:b * W], ind).then_inc(sem, 1)
-        else:
-            g.scalar.activation(out[:, a * W:b * W], ind, ActivationFunctionType.Copy).then_inc(sem, 1)
-
-    gsem = [S.ga, S.gb, S["gc_"]]
+    def gathers(out, src, groups, ready):
+        for k, q in enumerate((g.vector, g.scalar)):
+            for s, v in ready:
+                q.wait_ge(s, v)
+            for st, idx in enumerate(groups):
+                for a, b in runs(idx):
+                    mid = (a + b) * W // 32 * 16
+                    lo, hi = ((a * W, mid), (mid, b * W))[k]
+                    ind = src[:, :].indirect(T.off[:, lo // 16:hi // 16])
+                    if k == 0:
+                        q.tensor_copy(out[:, lo:hi], ind).then_inc(gsem[st], 1)
+                    else:
+                        q.activation(out[:, lo:hi], ind, ActivationFunctionType.Copy).then_inc(gsem[st], 1)
+        return [2 * len(runs(idx)) for idx in groups]
 
     if core in rank_core:
         pos = rank_core.index(core)
-        mu = inter[pos]
-        start, relays, calls, gathers = phase1(topo, pos, rank_core, inter, second)
-        low, high = engines(topo, core, rank_core)
+        start, relays, n, calls = phase1(topo, pos, rank_core, inter)
         g.sync.dma_start(T.xs[:], T.x[:]).then_inc(S.xl, 16)
         g.scalar.dma_start(T.h1[0:1, 0:2], T.hh[0:1, 0:2]).then_inc(S.hl, 16)
         g.iota(T.pi[:], [[0, 1]], 0, 1).then_inc(S.iop, 1)
-        g.iota(T.ia[:], [[16, NR * OC]], start * W, 0).then_inc(S.ioa, 1)
+        g.iota(T.ia[:], [[16, COLS // 16]], start * W, 0).then_inc(S.ioa, 1)
         g.wait_ge(S.hl, 16)
         g.partition_broadcast(T.hb[:], T.h1[0:1, 0:2], 128).then_inc(S.pb, 1)
         g.wait_ge(S.pb, 1)
-        rid, pid, _ = topo.addr(mu)
-        g.remote_dma(T.hb[:], T.hb[:], S.hland, S.rl, pid, rid, topo.mask(core, mu))
-        sent = count(topo.mask(core, mu))
+        fused([(m, e, 0) for m, e in feeds(topo, rank_core, inter)[core]], S.hland,
+              lambda k: T.hb[:], lambda k: T.hb[:])
+        v = g.vector
         lane()
-        g.vector.wait_ge(S.pb, 1)
-        g.vector.tensor_copy(T.hf[:], T.hb[:, 0:1]).then_inc(S.vc, 1)
-        g.vector.wait_ge(S.vc, 3)
-        g.vector.wait_ge(S.ioa, 1)
-        g.vector.tensor_scalar(T.ib[:], T.ia[:], T.pf[:], T.hf[:], AluOpType.add, AluOpType.add).then_inc(S.vc, 1)
-        g.vector.wait_ge(S.vc, 4)
-        g.vector.tensor_scalar(T.ic[:], T.ib[:], COLS - 1, None, AluOpType.bitwise_and).then_inc(S.vc, 1)
-        g.vector.wait_ge(S.vc, 5)
-        g.vector.tensor_copy(T.off[:], T.ic[:]).then_inc(S.vc, 1)
-        for k, q in enumerate((g.vector, g.scalar)):
-            q.wait_ge(S.vc, 6)
-            q.wait_ge(S.xl, 16)
-            for st, pair in enumerate(gathers):
-                gather(k, T.rot, T.xs, pair[k][0], pair[k][1], gsem[st])
-        g.wait_ge(gsem[0], 2)
-        widths = sorted({n for _, _, n, _ in relays})
-        for n in widths:
-            tr = [xfer(d, m, S.rland, cols(T.rot, i, n), cols(T.rel, 0, n)) for d, i, nn, m in relays if nn == n]
-            g.remote_dma_fused(tr, local_sem=S.rl)
-        sent += sum(count(m) for _, _, _, m in relays)
+        v.wait_ge(S.pb, 1)
+        v.tensor_copy(T.hf[:], T.hb[:, 0:1]).then_inc(S.vc, 1)
+        v.wait_ge(S.vc, 3)
+        v.wait_ge(S.ioa, 1)
+        v.tensor_scalar(T.ib[:], T.ia[:], T.pf[:], T.hf[:], AluOpType.add, AluOpType.add).then_inc(S.vc, 1)
+        v.wait_ge(S.vc, 4)
+        v.tensor_scalar(T.ic[:], T.ib[:], COLS - 1, None, AluOpType.bitwise_and).then_inc(S.vc, 1)
+        v.wait_ge(S.vc, 5)
+        v.tensor_copy(T.off[:], T.ic[:]).then_inc(S.vc, 1)
+        done = gathers(T.rot, T.xs, [range(n)] + [[i for i, _ in c] for c in calls], [(S.vc, 6), (S.xl, 16)])
+        g.wait_ge(gsem[0], done[0])
+        fused([(d, m, (i, k)) for d, i, k, m in relays], S.rland,
+              lambda k: cols(T.rot, k[0], k[1]), lambda k: cols(T.rel, 0, k[1]))
         slot = T.rank_of(core)
         for st, call in enumerate(calls):
-            g.wait_ge(gsem[st + 1], 2)
-            g.remote_dma_fused([xfer(inter[(start + i) % NR], m, S.wland, cols(T.rot, i), cols(T.win, slot))
-                                for i, m in call], local_sem=S.rl)
-            sent += sum(count(m) for _, m in call)
-        need = [0, 0]
-        half = [[], []]
-        for p in range(NR):
+            g.wait_ge(gsem[st + 1], done[st + 1])
+            fused([(inter[(start + i) % NI], m, i) for i, m in call], S.wland,
+                  lambda i: cols(T.rot, i), lambda i: cols(T.win, slot))
+        need = [0] * STEPS
+        got = [[] for _ in range(STEPS)]
+        for p in range(NI):
             s2, c2 = phase2(topo, p, rank_core, inter)
             for st, call in enumerate(c2):
                 for i, m in call:
                     if (s2 + i) % NR == pos:
-                        h = 0 if st < 2 else 1
-                        need[h] += count(m)
-                        half[h].append(p)
+                        need[st] += count(m)
+                        got[st].append(p)
         stores = 0
-        for h in range(2):
-            runs = []
-            for p in half[h]:
-                if runs and runs[-1][1] == p:
-                    runs[-1][1] = p + 1
-                else:
-                    runs.append([p, p + 1])
-            if len(runs) == 1:
-                a, b = runs[0]
-                runs = [[a, (a + b) // 2], [(a + b) // 2, b]]
-            for k, (a, b) in enumerate(runs):
+        for st in range(STEPS):
+            parts = runs(got[st])
+            if len(parts) == 1:
+                a, b = parts[0]
+                parts = [[a, (a + b) // 2], [(a + b) // 2, b]]
+            for k, (a, b) in enumerate(parts):
                 q = (g.sync, g.scalar)[k % 2]
-                q.wait_ge((S.z0, S.z1)[h], need[h])
+                q.wait_ge(zsem[st], need[st])
                 q.dma_start(T.y[:, a * W:b * W], T.land[:, a * W:b * W]).then_inc(S.st, 16)
                 stores += 16
-        g.wait_ge(S.rl, sent)
+        g.wait_ge(S.rl, sent[0])
         g.sync.wait_ge(S.st, stores)
         return
 
-    jobs = []
-    if core in inter or core in second:
-        for p in range(NR):
-            for d, i, n, m in phase1(topo, p, rank_core, inter, second)[1]:
-                if d == core:
-                    jobs.append((p, i, n, m))
-    if not jobs and core not in inter:
+    here, who = shares(topo, topo.chip(core), rank_core, inter)
+    if core not in who:
         return
-    sent = 0
+    jobs = []
+    for p in range(NR):
+        s1, relays, _, _ = phase1(topo, p, rank_core, inter)
+        jobs += [(p, s1, i, n, m) for d, i, n, m in relays if d == core]
+    start2 = phase2(topo, inter.index(here[0]), rank_core, inter)[0]
+    a, b = who[core]
+    dest = [rank_at[(start2 + i) % NR] for i in range(NR)]
+    made, i = 0, a
+    while i < b:
+        j = i + 1
+        while j < b and dest[j] - dest[j - 1] == dest[i + 1] - dest[i]:
+            j += 1
+        pat = [[16, OC]] if j == i + 1 else [[COLS * (dest[i + 1] - dest[i]), j - i], [16, OC]]
+        g.iota(T.tab[:, i * OC:j * OC], pat, COLS * dest[i], 0).then_inc(S.tm, 1)
+        made, i = made + 1, j
+    g.wait_ge(S.tm, made)
+    fused([(m, e, 0) for m, e in share_writes(topo, core, here)], S.tland,
+          lambda k: T.tab[:, a * OC:b * OC], lambda k: T.tab[:, a * OC:b * OC])
     if core in inter:
         pos = inter.index(core)
-        start2, calls2 = phase2(topo, pos, rank_core, inter)
+        calls2 = phase2(topo, pos, rank_core, inter)[1]
         g.iota(T.pi[:], [[0, 1]], 0, 1).then_inc(S.iop, 1)
         g.iota(T.it[:], [[0, NR], [16, OC]], 0, 0).then_inc(S.iot, 1)
-        for i in range(NR):
-            b = rank_at[(start2 + i) % NR]
-            g.iota(T.ia[:, i * OC:(i + 1) * OC], [[16, OC]], COLS * b + W * pos, 0).then_inc(S.ioa, 1)
-        lane()
         v = g.vector
-        v.wait_ge(S.hland, count(topo.mask(rank_core[pos], core)))
-        v.tensor_copy(T.hf[:], T.hb[:, 0:1]).then_inc(S.vc, 1)
+        lane()
         v.wait_ge(S.iot, 1)
-        v.wait_ge(S.vc, 3)
+        v.wait_ge(S.vc, 2)
         v.tensor_scalar(T.iu[:], T.it[:], T.pf[:], None, AluOpType.add).then_inc(S.vc, 1)
-        v.wait_ge(S.ioa, NR)
-        v.wait_ge(S.vc, 4)
-        v.tensor_scalar(T.ib[:], T.ia[:], T.pf[:], T.hf[:], AluOpType.add, AluOpType.add).then_inc(S.vc, 1)
+        v.wait_ge(S.tm, made)
+        v.wait_ge(S.tland, sum(count(e) for c in who for m, e in share_writes(topo, c, here) if m == core))
+        v.tensor_scalar(T.ib[:, 0:K], T.tab[:], T.pf[:], float(W * pos), AluOpType.add,
+                        AluOpType.add).then_inc(S.vc, 1)
+        v.wait_ge(S.hland, sum(count(e) for f in feeds(topo, rank_core, inter).values() for m, e in f if m == core))
+        v.tensor_copy(T.hf[:], T.hb[:, 0:1]).then_inc(S.vc, 1)
         v.wait_ge(S.vc, 5)
-        v.tensor_scalar(T.ic[:], T.ib[:], 11, NR - 1, AluOpType.logical_shift_right,
-                        AluOpType.bitwise_and).then_inc(S.vc, 1)
+        v.tensor_scalar(T.ic[:, 0:K], T.ib[:, 0:K], T.hf[:], None, AluOpType.add).then_inc(S.vc, 1)
         v.wait_ge(S.vc, 6)
-        v.tensor_scalar(T["id_"][:], T.ic[:], float(W), None, AluOpType.mult).then_inc(S.vc, 1)
+        v.tensor_scalar(T["id_"][:], T.ic[:, 0:K], 11 - (W.bit_length() - 1), (NR - 1) * W,
+                        AluOpType.logical_shift_right, AluOpType.bitwise_and).then_inc(S.vc, 1)
         v.wait_ge(S.vc, 7)
         v.tensor_tensor(T.ie[:], T["id_"][:], T.iu[:], AluOpType.add).then_inc(S.vc, 1)
         v.wait_ge(S.vc, 8)
-        v.tensor_copy(T.off[:], T.ie[:]).then_inc(S.vc, 1)
+        v.tensor_copy(T.off[:, 0:K], T.ie[:]).then_inc(S.vc, 1)
         need = 0
         for p in range(NR):
-            s1, rl1, c1, _ = phase1(topo, p, rank_core, inter, second)
-            todo = [c for c in c1]
-            for d, i, n, _m in rl1:
-                todo += relay_calls(topo, d, i, n, rank_core)
-            need += sum(count(m) for c in todo for i, m in c if (s1 + i) % NR == pos)
-        for k, q in enumerate((g.vector, g.scalar)):
-            q.wait_ge(S.vc, 9)
-            q.wait_ge(S.wland, need)
-            for st, (a, b) in enumerate(((0, 4), (4, 8), (8, 16))):
-                mid = (a + b) // 2
-                gather(k, T.sel, T.win, (a, mid)[k], (mid, b)[k], gsem[st])
-    for p, first, n, mask in jobs:
+            s1, relays, _, todo = phase1(topo, p, rank_core, inter)
+            for d, i, n, _m in relays:
+                todo = todo + relay_calls(topo, d, s1, i, n, inter)
+            need += sum(count(m) for c in todo for i, m in c if (s1 + i) % NI == pos)
+        done = gathers(T.sel, T.win, [[i for i, _ in c] for c in calls2], [(S.vc, 9), (S.wland, need)])
+    for p, s1, first, n, mask in jobs:
         g.wait_ge(S.rland, count(mask))
-        s1 = phase1(topo, p, rank_core, inter, second)[0]
-        for call in relay_calls(topo, core, first, n, rank_core):
-            g.remote_dma_fused([xfer(inter[(s1 + i) % NR], m, S.wland, cols(T.rel, i - first), cols(T.win, rank_at[p]))
-                                for i, m in call], local_sem=S.rl)
-            sent += sum(count(m) for _, m in call)
+        for call in relay_calls(topo, core, s1, first, n, inter):
+            fused([(inter[(s1 + i) % NI], m, i) for i, m in call], S.wland,
+                  lambda i: cols(T.rel, i - first), lambda i: cols(T.win, rank_at[p]))
     if core in inter:
         for st, call in enumerate(calls2):
-            g.wait_ge(gsem[st], 2)
-            g.remote_dma_fused([xfer(rank_core[(start2 + i) % NR], m, (S.z0, S.z1)[0 if st < 2 else 1],
-                                     cols(T.sel, i), cols(T.land, pos)) for i, m in call], local_sem=S.rl)
-            sent += sum(count(m) for _, m in call)
-    g.wait_ge(S.rl, sent)
+            g.wait_ge(gsem[st], done[st])
+            fused([(rank_core[(start2 + i) % NR], m, i) for i, m in call], zsem[st],
+                  lambda i: cols(T.sel, i), lambda i: cols(T.land, pos))
+    g.wait_ge(S.rl, sent[0])

from concourse.bass import DstId, RemoteDMATransfer
from concourse.mybir import AluOpType, ActivationFunctionType

NR = 16
NI = 32
COLS = 2048
W = COLS // NI
OC = W // 16
K = NR * OC
RELAY = 8
STEPS = 4

SCRATCH = {
    "xs": ("sbuf", [128, COLS], "bfloat16"),
    "rot": ("sbuf", [128, COLS], "bfloat16"),
    "rel": ("sbuf", [128, COLS], "bfloat16"),
    "win": ("sbuf", [128, NR * W], "bfloat16"),
    "sel": ("sbuf", [128, NR * W], "bfloat16"),
    "land": ("sbuf", [128, COLS], "bfloat16"),
    "h1": ("sbuf", [128, 2], "int32"),
    "hb": ("sbuf", [128, 2], "int32"),
    "hf": ("sbuf", [128, 1], "float32"),
    "pi": ("sbuf", [128, 1], "int32"),
    "pj": ("sbuf", [128, 1], "int32"),
    "pf": ("sbuf", [128, 1], "float32"),
    "ia": ("sbuf", [128, COLS // 16], "int32"),
    "ib": ("sbuf", [128, COLS // 16], "int32"),
    "ic": ("sbuf", [128, COLS // 16], "int32"),
    "id_": ("sbuf", [128, K], "int32"),
    "ie": ("sbuf", [128, K], "int32"),
    "it": ("sbuf", [128, K], "int32"),
    "iu": ("sbuf", [128, K], "int32"),
    "tab": ("sbuf", [128, K], "int32"),
    "off": ("sbuf", [128, COLS // 16], "uint16"),
}
SEMAPHORES = ["xl", "hl", "pb", "iop", "ioa", "iot", "vc", "tm", "tland", "rl", "hland", "rland", "wland", "st",
              "g0", "g1", "g2", "g3", "g4", "z0", "z1", "z2", "z3"]


def bits(m):
    return [1 << i for i in range(m.bit_length()) if (m >> i) & 1]


def count(mask):
    return len(bits(mask))


def pow2(n):
    return 1 << (n - 1).bit_length()


def deal(engines, n):
    k = len(engines) // n
    return [sum(engines[i * k:(i + 1) * k]) for i in range(n)]


def runs(idx):
    out = []
    for i in sorted(idx):
        if out and out[-1][1] == i:
            out[-1][1] = i + 1
        else:
            out.append([i, i + 1])
    return out


def cols(t, i, n=1):
    return t[:, i * W:(i + n) * W]


def all_cores(topo):
    return range(topo.CHIPS * topo.CORES_PER_CHIP)


def layout(T, topo):
    cores = list(T.cores)
    planes = []
    for ch in range(topo.CHIPS):
        for p in planes:
            if topo.same_plane(ch, p[0]):
                p.append(ch)
                break
        else:
            planes.append([ch])
    order = [ch for p in planes for ch in p]
    rank_core = [c for ch in order for c in cores if topo.chip(c) == ch]
    dies = sorted({topo.die(c) for c in all_cores(topo)}, reverse=True)
    inter = [next(c for c in all_cores(topo) if topo.chip(c) == ch and topo.die(c) == d and c not in cores
                  and all(topo.may_write(c, r) for r in cores)) for ch in order for d in dies]
    return rank_core, inter


def engines(topo, core):
    on = bits(topo.mask(core, next(c for c in all_cores(topo) if topo.chip(c) == topo.chip(core) and c != core)))
    off = bits(topo.mask(core, next(c for c in all_cores(topo) if topo.same_plane(topo.chip(c), topo.chip(core)))))
    return off, [e for e in on if e not in off]


def calls_for(topo, core, dst, idx, sizes):
    low, high = engines(topo, core)
    on = [i for i in idx if topo.chip(dst(i)) == topo.chip(core)]
    off = [i for i in idx if i not in on]
    calls, k = [], 0
    for s in sizes(len(off)):
        calls.append(list(zip(off[k:k + s], deal(low, s))))
        k += s
    if on:
        calls[0] += list(zip(on, deal(high, pow2(len(on)))))
    return calls


def wide(n):
    return [s for s in (1, 2, 4) if n & s] + [8] * (n // 8)


def stepwise(n):
    return ([n % 4] if n % 4 else []) + [4] * (n // 4)


def phase1(topo, pos, rank_core, inter):
    core = rank_core[pos]
    chip = topo.chip(core)
    low, high = engines(topo, core)
    mine = [d for d in all_cores(topo) if topo.chip(d) == chip and topo.die(d) == topo.die(core)
            and d not in rank_core]
    full = [d for d in mine if all(topo.may_write(d, r) for r in rank_core)]
    part = [d for d in mine if d not in full]
    other = [p for p in range(NI) if topo.chip(inter[p]) != chip and not topo.same_plane(topo.chip(inter[p]), chip)]
    barred = [p for p in range(NI) if not topo.may_write(core, inter[p])]
    if barred:
        start, n = barred[0], len(barred)
        k = n // len(full)
        parts = [(d, j * k, k) for j, d in enumerate(full)]
    else:
        start, n = other[-1] + 1 - RELAY, 2 * RELAY
        parts = [(full[0], 0, RELAY), (part[0], RELAY, RELAY)]
    relays = [(d, i, k, m) for (d, i, k), m in zip(parts, deal(low + high, len(parts)))]
    return start, relays, n, calls_for(topo, core, lambda i: inter[(start + i) % NI], range(n, NI), wide)


def relay_calls(topo, helper, start, first, n, inter):
    return calls_for(topo, helper, lambda i: inter[(start + i) % NI], range(first, first + n), wide)


def phase2(topo, pos, rank_core, inter):
    chip = topo.chip(inter[pos])
    key = [topo.chip(c) for c in rank_core]
    if chip in key:
        start = key.index(chip)
    else:
        idle = []
        for m in inter:
            if topo.chip(m) not in key and topo.chip(m) not in idle:
                idle.append(topo.chip(m))
        idle.sort()
        start = idle.index(chip) * NR // len(idle)
    return start, calls_for(topo, inter[pos], lambda i: rank_core[(start + i) % NR], range(NR), stepwise)


def feeds(topo, rank_core, inter):
    out = {c: [] for c in rank_core}
    rest = []
    for m in inter:
        own = [c for c in rank_core if topo.chip(c) == topo.chip(m) and topo.die(c) == topo.die(m)]
        if own:
            out[own[0]].append(m)
        else:
            rest.append(m)
    for m in rest:
        able = [c for c in rank_core if topo.may_write(c, m)]
        out[min(able, key=lambda c: (len(out[c]), all(topo.may_write(c, i) for i in inter)))].append(m)
    for c in rank_core:
        low, high = engines(topo, c)
        on = [m for m in out[c] if topo.chip(m) == topo.chip(c)]
        off = [m for m in out[c] if m not in on]
        out[c] = list(zip(on, deal(high, pow2(len(on))))) + (list(zip(off, deal(low, pow2(len(off))))) if off else [])
    return out


def shares(topo, chip, rank_core, inter):
    here = [c for c in inter if topo.chip(c) == chip]
    who = set(here)
    for p in range(NR):
        who |= {d for d, _, _, _ in phase1(topo, p, rank_core, inter)[1] if topo.chip(d) == chip}
    who = sorted(who)
    return here, {c: (k * NR // len(who), (k + 1) * NR // len(who)) for k, c in enumerate(who)}


def share_writes(topo, core, here):
    to = [m for m in here if m != core]
    return list(zip(to, deal(engines(topo, core)[0], len(to))))


def rank_program(g, core, T, topo):
    rank_core, inter = layout(T, topo)
    rank_at = [T.rank_of(c) for c in rank_core]
    S = T.sem
    gsem = [S["g%d" % k] for k in range(5)]
    zsem = [S["z%d" % k] for k in range(STEPS)]
    sent = [0]

    def fused(parts, sem, src, dst):
        tr = []
        for d, mask, k in parts:
            rid, pid, _ = topo.addr(d)
            tr.append(RemoteDMATransfer(dst_ids=[DstId(rid=rid, pnc=pid)], dma_engine_mask=mask, remote_sem=sem,
                                        src=src(k), dst=dst(k)))
            sent[0] += count(mask)
        g.remote_dma_fused(tr, local_sem=S.rl)

    def lane():
        g.vector.wait_ge(S.iop, 1)
        g.vector.tensor_scalar(T.pj[:], T.pi[:], 15, None, AluOpType.bitwise_and).then_inc(S.vc, 1)
        g.vector.wait_ge(S.vc, 1)
        g.vector.tensor_copy(T.pf[:], T.pj[:]).then_inc(S.vc, 1)

    def gathers(out, src, groups, ready):
        for k, q in enumerate((g.vector, g.scalar)):
            for s, v in ready:
                q.wait_ge(s, v)
            for st, idx in enumerate(groups):
                for a, b in runs(idx):
                    mid = (a + b) * W // 32 * 16
                    lo, hi = ((a * W, mid), (mid, b * W))[k]
                    ind = src[:, :].indirect(T.off[:, lo // 16:hi // 16])
                    if k == 0:
                        q.tensor_copy(out[:, lo:hi], ind).then_inc(gsem[st], 1)
                    else:
                        q.activation(out[:, lo:hi], ind, ActivationFunctionType.Copy).then_inc(gsem[st], 1)
        return [2 * len(runs(idx)) for idx in groups]

    if core in rank_core:
        pos = rank_core.index(core)
        start, relays, n, calls = phase1(topo, pos, rank_core, inter)
        g.sync.dma_start(T.xs[:], T.x[:]).then_inc(S.xl, 16)
        g.scalar.dma_start(T.h1[0:1, 0:2], T.hh[0:1, 0:2]).then_inc(S.hl, 16)
        g.iota(T.pi[:], [[0, 1]], 0, 1).then_inc(S.iop, 1)
        g.iota(T.ia[:], [[16, COLS // 16]], start * W, 0).then_inc(S.ioa, 1)
        g.wait_ge(S.hl, 16)
        g.partition_broadcast(T.hb[:], T.h1[0:1, 0:2], 128).then_inc(S.pb, 1)
        g.wait_ge(S.pb, 1)
        fused([(m, e, 0) for m, e in feeds(topo, rank_core, inter)[core]], S.hland,
              lambda k: T.hb[:], lambda k: T.hb[:])
        v = g.vector
        lane()
        v.wait_ge(S.pb, 1)
        v.tensor_copy(T.hf[:], T.hb[:, 0:1]).then_inc(S.vc, 1)
        v.wait_ge(S.vc, 3)
        v.wait_ge(S.ioa, 1)
        v.tensor_scalar(T.ib[:], T.ia[:], T.pf[:], T.hf[:], AluOpType.add, AluOpType.add).then_inc(S.vc, 1)
        v.wait_ge(S.vc, 4)
        v.tensor_scalar(T.ic[:], T.ib[:], COLS - 1, None, AluOpType.bitwise_and).then_inc(S.vc, 1)
        v.wait_ge(S.vc, 5)
        v.tensor_copy(T.off[:], T.ic[:]).then_inc(S.vc, 1)
        done = gathers(T.rot, T.xs, [range(n)] + [[i for i, _ in c] for c in calls], [(S.vc, 6), (S.xl, 16)])
        g.wait_ge(gsem[0], done[0])
        fused([(d, m, (i, k)) for d, i, k, m in relays], S.rland,
              lambda k: cols(T.rot, k[0], k[1]), lambda k: cols(T.rel, 0, k[1]))
        slot = T.rank_of(core)
        for st, call in enumerate(calls):
            g.wait_ge(gsem[st + 1], done[st + 1])
            fused([(inter[(start + i) % NI], m, i) for i, m in call], S.wland,
                  lambda i: cols(T.rot, i), lambda i: cols(T.win, slot))
        need = [0] * STEPS
        got = [[] for _ in range(STEPS)]
        for p in range(NI):
            s2, c2 = phase2(topo, p, rank_core, inter)
            for st, call in enumerate(c2):
                for i, m in call:
                    if (s2 + i) % NR == pos:
                        need[st] += count(m)
                        got[st].append(p)
        stores = 0
        for st in range(STEPS):
            parts = runs(got[st])
            if len(parts) == 1:
                a, b = parts[0]
                parts = [[a, (a + b) // 2], [(a + b) // 2, b]]
            for k, (a, b) in enumerate(parts):
                q = (g.sync, g.scalar)[k % 2]
                q.wait_ge(zsem[st], need[st])
                q.dma_start(T.y[:, a * W:b * W], T.land[:, a * W:b * W]).then_inc(S.st, 16)
                stores += 16
        g.wait_ge(S.rl, sent[0])
        g.sync.wait_ge(S.st, stores)
        return

    here, who = shares(topo, topo.chip(core), rank_core, inter)
    if core not in who:
        return
    jobs = []
    for p in range(NR):
        s1, relays, _, _ = phase1(topo, p, rank_core, inter)
        jobs += [(p, s1, i, n, m) for d, i, n, m in relays if d == core]
    start2 = phase2(topo, inter.index(here[0]), rank_core, inter)[0]
    a, b = who[core]
    dest = [rank_at[(start2 + i) % NR] for i in range(NR)]
    made, i = 0, a
    while i < b:
        j = i + 1
        while j < b and dest[j] - dest[j - 1] == dest[i + 1] - dest[i]:
            j += 1
        pat = [[16, OC]] if j == i + 1 else [[COLS * (dest[i + 1] - dest[i]), j - i], [16, OC]]
        g.iota(T.tab[:, i * OC:j * OC], pat, COLS * dest[i], 0).then_inc(S.tm, 1)
        made, i = made + 1, j
    g.wait_ge(S.tm, made)
    fused([(m, e, 0) for m, e in share_writes(topo, core, here)], S.tland,
          lambda k: T.tab[:, a * OC:b * OC], lambda k: T.tab[:, a * OC:b * OC])
    if core in inter:
        pos = inter.index(core)
        calls2 = phase2(topo, pos, rank_core, inter)[1]
        g.iota(T.pi[:], [[0, 1]], 0, 1).then_inc(S.iop, 1)
        g.iota(T.it[:], [[0, NR], [16, OC]], 0, 0).then_inc(S.iot, 1)
        v = g.vector
        lane()
        v.wait_ge(S.iot, 1)
        v.wait_ge(S.vc, 2)
        v.tensor_scalar(T.iu[:], T.it[:], T.pf[:], None, AluOpType.add).then_inc(S.vc, 1)
        v.wait_ge(S.tm, made)
        v.wait_ge(S.tland, sum(count(e) for c in who for m, e in share_writes(topo, c, here) if m == core))
        v.tensor_scalar(T.ib[:, 0:K], T.tab[:], T.pf[:], float(W * pos), AluOpType.add,
                        AluOpType.add).then_inc(S.vc, 1)
        v.wait_ge(S.hland, sum(count(e) for f in feeds(topo, rank_core, inter).values() for m, e in f if m == core))
        v.tensor_copy(T.hf[:], T.hb[:, 0:1]).then_inc(S.vc, 1)
        v.wait_ge(S.vc, 5)
        v.tensor_scalar(T.ic[:, 0:K], T.ib[:, 0:K], T.hf[:], None, AluOpType.add).then_inc(S.vc, 1)
        v.wait_ge(S.vc, 6)
        v.tensor_scalar(T["id_"][:], T.ic[:, 0:K], 11 - (W.bit_length() - 1), (NR - 1) * W,
                        AluOpType.logical_shift_right, AluOpType.bitwise_and).then_inc(S.vc, 1)
        v.wait_ge(S.vc, 7)
        v.tensor_tensor(T.ie[:], T["id_"][:], T.iu[:], AluOpType.add).then_inc(S.vc, 1)
        v.wait_ge(S.vc, 8)
        v.tensor_copy(T.off[:, 0:K], T.ie[:]).then_inc(S.vc, 1)
        need = 0
        for p in range(NR):
            s1, relays, _, todo = phase1(topo, p, rank_core, inter)
            for d, i, n, _m in relays:
                todo = todo + relay_calls(topo, d, s1, i, n, inter)
            need += sum(count(m) for c in todo for i, m in c if (s1 + i) % NI == pos)
        done = gathers(T.sel, T.win, [[i for i, _ in c] for c in calls2], [(S.vc, 9), (S.wland, need)])
    for p, s1, first, n, mask in jobs:
        g.wait_ge(S.rland, count(mask))
        for call in relay_calls(topo, core, s1, first, n, inter):
            fused([(inter[(s1 + i) % NI], m, i) for i, m in call], S.wland,
                  lambda i: cols(T.rel, i - first), lambda i: cols(T.win, rank_at[p]))
    if core in inter:
        for st, call in enumerate(calls2):
            g.wait_ge(gsem[st], done[st])
            fused([(rank_core[(start2 + i) % NR], m, i) for i, m in call], zsem[st],
                  lambda i: cols(T.sel, i), lambda i: cols(T.land, pos))
    g.wait_ge(S.rl, sent[0])
